import numpy as np
import ml_dtypes


def mxq(x, axis, fmt="e4m3"):
    dtype, down = {"e4m3": (ml_dtypes.float8_e4m3fn, 7), "e5m2": (ml_dtypes.float8_e5m2, 14)}[fmt]
    v = np.moveaxis(np.asarray(x, np.float32).astype(ml_dtypes.bfloat16).astype(np.float64), axis, -1)
    blocks = v.reshape(v.shape[:-1] + (-1, 32))
    amax = np.abs(blocks).max(-1, keepdims=True)
    byte = np.maximum(np.where(amax > 0, np.frexp(amax)[1] - 1 + 127, 0) - down, 1)
    scale = np.exp2(byte - 127.0)
    codes = (blocks / scale).astype(np.float32).astype(dtype).astype(np.float64)
    return np.moveaxis((codes * scale).reshape(v.shape), -1, axis)


WIDE = False


def mx_kscale(k):
    if not WIDE:
        return np.ones(k)
    levels = np.array([10, -10, 5, -5, 0])
    if k % 512:
        return np.exp2(np.random.permutation(np.resize(levels, k // 32))).repeat(32)
    a = np.empty((k // 512, 16))
    for p in range(k // 512):
        a[p, :8] = np.random.permutation(np.resize(levels, 8))
        for g in range(8):
            far = levels[np.abs(levels - a[p, g]) >= 10]
            a[p, g + 8] = far[np.random.randint(len(far))]
    return np.exp2(a.ravel()).repeat(32)


def f64(x):
    return np.asarray(x).astype(np.float64)


def striped(idx):
    return np.tile(idx.reshape(-1, 16).T, (8, 1)).astype(np.uint16)


def unstriped(offs):
    return offs[:16].T.reshape(-1).astype(np.int64)


K, T, S, V, N = 1024, 2048, 512, 128, 128


def setup_inputs():
    n = np.random.standard_normal
    s = mx_kscale(K)[:, None]
    return {
        "xT": (n((K, T)) * s).astype(np.float32),
        "w1": (n((K, N)) / np.sqrt(K) / s).astype(np.float32),
        "w2": (n((K, N)) / np.sqrt(K) / s).astype(np.float32),
        "offs": striped(np.random.permutation(T)[:S]),
    }


def reference(xT, w1, w2, offs):
    xq = mxq(f64(xT)[:, unstriped(offs)], 0, "e4m3")
    e = np.exp(mxq(f64(w1), 0, "e4m3").T @ xq)
    h = mxq(f64(w2), 0, "e4m3").T @ xq
    num = e[:, :V] * h[:, :V] + e[:, V:2 * V] * h[:, V:2 * V] + e[:, 2 * V:3 * V] * h[:, 2 * V:3 * V] + e[:, 3 * V:4 * V] * h[:, 3 * V:4 * V]
    den = e[:, :V] + e[:, V:2 * V] + e[:, 2 * V:3 * V] + e[:, 3 * V:4 * V]
    return num / den

@@ -1,0 +1,160 @@
+from contextlib import ExitStack
+
+import concourse.mybir as mybir
+
+K, T, S, V, N = 1024, 2048, 512, 128, 128
+FLOPS = 2 * 2 * K * N * S
+
+F32 = mybir.dt.float32
+BF16 = mybir.dt.bfloat16
+U32 = mybir.dt.uint32
+U16 = mybir.dt.uint16
+U8 = mybir.dt.uint8
+FP8X4 = mybir.dt.float8_e4m3fn_x4
+ALU = mybir.AluOpType
+ACT = mybir.ActivationFunctionType
+AX = mybir.AxisListType
+
+P = 128
+PACK = 4
+PASSES = K // (P * PACK)
+D = S // V
+HALVES = 2
+VH = V // HALVES
+SH = S // HALVES
+
+
+def tile_picked_apool_none_e_kernel(tc, xT, w1, w2, offs, out):
+    nc = tc.nc
+    with ExitStack() as ctx:
+        keep = ctx.enter_context(tc.tile_pool(name="keep", bufs=1))
+        psum = ctx.enter_context(tc.psum_pool(name="psum", bufs=1))
+
+        offsets = keep.tile([P, S // 16], U16, name="offsets")
+        x_rows = xT.rearrange("(g p j) t -> g j p t", g=PASSES, j=PACK)
+        planes = {}
+        for g in range(PASSES):
+            for j in range(PACK):
+                planes[g, j] = keep.tile([P, T], F32, name="plane%d_%d" % (g, j))
+                nc.sync.dma_start(out=planes[g, j][:], in_=x_rows[g, j])
+                if (g, j) == (0, 0):
+                    nc.sync.dma_start(offsets[:], offs)
+        w_raw = {}
+        for i, w in enumerate((w1, w2)):
+            w_rows = w.rearrange("(g p j) n -> g p j n", g=PASSES, j=PACK)
+            for g in range(PASSES):
+                w_raw[i, g] = keep.tile([P, PACK, N], F32, name="w_raw%d_%d" % (i, g))
+                nc.sync.dma_start(out=w_raw[i, g][:], in_=w_rows[g])
+
+        warm_in = keep.tile([P, 1], F32, name="warm_in")
+        warm_out = keep.tile([P, 1], F32, name="warm_out")
+        nc.vector.memset(warm_in[:], 0.0)
+        nc.scalar.activation(out=warm_out[:], in_=warm_in[:], func=ACT.Exp)
+
+        def quantize(name, src, width):
+            codes = keep.tile([P, width], U32, name=name + "_codes", align_bytes=64)
+            scales = keep.tile([P, width], U8, name=name + "_scales", align_bytes=64)
+            nc.vector.quantize_mx(out=codes[:].bitcast(FP8X4), scales=scales[:], in_=src)
+            return codes, scales
+
+        def gather(g):
+            picked = keep.tile([P, S, PACK], BF16, name="picked%d" % g, align_bytes=64)
+            by_entry = picked[:].rearrange("p (h d v) j -> p j d h v", h=HALVES, d=D)
+            for j in range(PACK):
+                nc.vector.tensor_copy(by_entry[:, j], planes[g, j][:].indirect(offsets[:]))
+            return picked[:].rearrange("p s j -> p (s j)")
+
+        def round_w(i, g):
+            grouped = keep.tile([P, N, PACK], BF16, name="w_bf%d_%d" % (i, g), align_bytes=64)
+            nc.scalar.copy(
+                out=grouped[:].rearrange("p (c i) j -> p c j i", i=4),
+                in_=w_raw[i, g][:].rearrange("p j (c i) -> p c j i", i=4),
+            )
+            return grouped[:].rearrange("p n j -> p (n j)")
+
+        xq = {}
+        picked0 = gather(0)
+        c0, s0 = quantize("x0", picked0, S)
+        for h in range(HALVES):
+            xq[0, h] = (c0[:, h * SH : (h + 1) * SH], s0[:, h * SH : (h + 1) * SH])
+        picked1 = gather(1)
+        w_bf = {(i, g): round_w(i, g) for i in range(2) for g in range(PASSES)}
+        wq = {}
+
+        def quantize_x1(h):
+            c, s = quantize("x1_%d" % h, picked1[:, h * SH * PACK : (h + 1) * SH * PACK], SH)
+            xq[1, h] = (c[:], s[:])
+
+        def quantize_w(i, g):
+            wq[i, g] = quantize("w%d_%d" % (i, g), w_bf[i, g], N)
+
+        acc = {(i, h): psum.tile([P, SH], F32, name="acc%d_%d" % (i, h)) for i in range(2) for h in range(HALVES)}
+
+        def product(i, g, h):
+            nc.tensor.matmul_mx(
+                out=acc[i, h][:],
+                lhsT=wq[i, g][0][:].bitcast(FP8X4),
+                lhsT_scale=wq[i, g][1][:],
+                rhs=xq[g, h][0].bitcast(FP8X4),
+                rhs_scale=xq[g, h][1],
+                start=(g == 0),
+                stop=(g == PASSES - 1),
+            )
+
+        quantize_w(0, 0)
+        product(0, 0, 0)
+        product(0, 0, 1)
+        quantize_x1(0)
+        quantize_w(0, 1)
+        product(0, 1, 0)
+        quantize_x1(1)
+        product(0, 1, 1)
+        quantize_w(1, 0)
+        product(1, 0, 0)
+        product(1, 0, 1)
+
+        top = {}
+        for h in range(HALVES):
+            top[h] = keep.tile([P, VH], F32, name="top%d" % h)
+            nc.vector.tensor_reduce(
+                out=top[h][:], in_=acc[0, h][:].rearrange("p (d v) -> p v d", d=D), axis=AX.X, op=ALU.max
+            )
+            if h == 0:
+                quantize_w(1, 1)
+                product(1, 1, 0)
+                product(1, 1, 1)
+        terms = {}
+        for h in range(HALVES):
+            shifted = keep.tile([P, D, VH], F32, name="shifted%d" % h)
+            nc.vector.tensor_tensor(
+                out=shifted[:],
+                in0=acc[0, h][:].rearrange("p (d v) -> p d v", d=D),
+                in1=top[h][:].unsqueeze(1).to_broadcast([P, D, VH]),
+                op=ALU.subtract,
+            )
+            terms[h] = keep.tile([P, 2, SH], F32, name="terms%d" % h)
+            nc.scalar.activation(out=terms[h][:, 0, :], in_=shifted[:].rearrange("p d v -> p (d v)"), func=ACT.Exp)
+        for h in range(HALVES):
+            nc.vector.tensor_tensor(out=terms[h][:, 1, :], in0=acc[1, h][:], in1=terms[h][:, 0, :], op=ALU.mult)
+        pairs = {}
+        for h in range(HALVES):
+            pairs[h] = keep.tile([P, 2, 2 * VH], F32, name="pairs%d" % h)
+            nc.vector.tensor_tensor(
+                out=pairs[h][:], in0=terms[h][:, :, : 2 * VH], in1=terms[h][:, :, 2 * VH :], op=ALU.add
+            )
+        sums = {}
+        for h in range(HALVES):
+            sums[h] = keep.tile([P, 2, VH], F32, name="sums%d" % h)
+            nc.vector.tensor_tensor(out=sums[h][:], in0=pairs[h][:, :, :VH], in1=pairs[h][:, :, VH:], op=ALU.add)
+        both = keep.tile([P, VH], F32, name="both")
+        nc.vector.tensor_tensor(out=both[:], in0=sums[0][:, 0, :], in1=sums[1][:, 0, :], op=ALU.mult)
+        cross = keep.tile([P, HALVES, VH], F32, name="cross")
+        nc.vector.tensor_tensor(out=cross[:, 0, :], in0=sums[0][:, 1, :], in1=sums[1][:, 0, :], op=ALU.mult)
+        rec = keep.tile([P, VH], F32, name="rec")
+        nc.vector.reciprocal(out=rec[:], in_=both[:])
+        nc.vector.tensor_tensor(out=cross[:, 1, :], in0=sums[1][:, 1, :], in1=sums[0][:, 0, :], op=ALU.mult)
+        res = keep.tile([P, HALVES, VH], F32, name="res")
+        nc.vector.tensor_tensor(
+            out=res[:], in0=cross[:], in1=rec[:].unsqueeze(1).to_broadcast([P, HALVES, VH]), op=ALU.mult
+        )
+        nc.sync.dma_start(out=out, in_=res[:].rearrange("p h v -> p (h v)"))

@@ -19,7 +19,11 @@ P = 128
 PACK = 4
 PASSES = K // (P * PACK)
 D = S // V
+PARTS = 4
+VP = V // PARTS
+SP = S // PARTS
 HALVES = 2
+PH = PARTS // HALVES
 VH = V // HALVES
 SH = S // HALVES
 
@@ -43,7 +47,7 @@ def tile_picked_apool_none_e_kernel(tc, xT, w1, w2, offs, out):
         for i, w in enumerate((w1, w2)):
             w_rows = w.rearrange("(g p j) n -> g p j n", g=PASSES, j=PACK)
             for g in range(PASSES):
-                w_raw[i, g] = keep.tile([P, PACK, N], F32, name="w_raw%d_%d" % (i, g))
+                w_raw[i, g] = keep.tile([P, PACK, N], F32, name="w_raw%d_%d" % (i, g), align_bytes=64)
                 nc.sync.dma_start(out=w_raw[i, g][:], in_=w_rows[g])
 
         warm_in = keep.tile([P, 1], F32, name="warm_in")
@@ -51,15 +55,9 @@ def tile_picked_apool_none_e_kernel(tc, xT, w1, w2, offs, out):
         nc.vector.memset(warm_in[:], 0.0)
         nc.scalar.activation(out=warm_out[:], in_=warm_in[:], func=ACT.Exp)
 
-        def quantize(name, src, width):
-            codes = keep.tile([P, width], U32, name=name + "_codes", align_bytes=64)
-            scales = keep.tile([P, width], U8, name=name + "_scales", align_bytes=64)
-            nc.vector.quantize_mx(out=codes[:].bitcast(FP8X4), scales=scales[:], in_=src)
-            return codes, scales
-
         def gather(g):
             picked = keep.tile([P, S, PACK], BF16, name="picked%d" % g, align_bytes=64)
-            by_entry = picked[:].rearrange("p (h d v) j -> p j d h v", h=HALVES, d=D)
+            by_entry = picked[:].rearrange("p (q d v) j -> p j d q v", q=PARTS, d=D)
             for j in range(PACK):
                 nc.vector.tensor_copy(by_entry[:, j], planes[g, j][:].indirect(offsets[:]))
             return picked[:].rearrange("p s j -> p (s j)")
@@ -72,89 +70,121 @@ def tile_picked_apool_none_e_kernel(tc, xT, w1, w2, offs, out):
             )
             return grouped[:].rearrange("p n j -> p (n j)")
 
-        xq = {}
+        x_codes, x_scales = {}, {}
         picked0 = gather(0)
-        c0, s0 = quantize("x0", picked0, S)
-        for h in range(HALVES):
-            xq[0, h] = (c0[:, h * SH : (h + 1) * SH], s0[:, h * SH : (h + 1) * SH])
+        x_codes[0] = keep.tile([P, S], U32, name="x_codes0", align_bytes=64)
+        x_scales[0] = keep.tile([P, S], U8, name="x_scales0", align_bytes=64)
+        nc.vector.quantize_mx(out=x_codes[0][:].bitcast(FP8X4), scales=x_scales[0][:], in_=picked0)
         picked1 = gather(1)
         w_bf = {(i, g): round_w(i, g) for i in range(2) for g in range(PASSES)}
+        x_codes[1] = keep.tile([P, S], U32, name="x_codes1", align_bytes=64, tag="w_raw0_1")
+        x_scales[1] = keep.tile([P, S], U8, name="x_scales1", align_bytes=64)
         wq = {}
 
-        def quantize_x1(h):
-            c, s = quantize("x1_%d" % h, picked1[:, h * SH * PACK : (h + 1) * SH * PACK], SH)
-            xq[1, h] = (c[:], s[:])
+        def quantize_x1(q):
+            cols = slice(q * SP, (q + 1) * SP)
+            nc.vector.quantize_mx(
+                out=x_codes[1][:, cols].bitcast(FP8X4),
+                scales=x_scales[1][:, cols],
+                in_=picked1[:, q * SP * PACK : (q + 1) * SP * PACK],
+            )
 
         def quantize_w(i, g):
-            wq[i, g] = quantize("w%d_%d" % (i, g), w_bf[i, g], N)
+            codes = keep.tile([P, N], U32, name="w_codes%d_%d" % (i, g), align_bytes=64)
+            scales = keep.tile([P, N], U8, name="w_scales%d_%d" % (i, g), align_bytes=64)
+            nc.vector.quantize_mx(out=codes[:].bitcast(FP8X4), scales=scales[:], in_=w_bf[i, g])
+            wq[i, g] = (codes, scales)
 
-        acc = {(i, h): psum.tile([P, SH], F32, name="acc%d_%d" % (i, h)) for i in range(2) for h in range(HALVES)}
+        score = [psum.tile([P, SP], F32, name="score%d" % q) for q in range(PARTS)]
+        value = [psum.tile([P, SH], F32, name="value%d" % h) for h in range(HALVES)]
 
-        def product(i, g, h):
+        def product(acc, i, g, part, width):
+            cols = slice(part * width, (part + 1) * width)
             nc.tensor.matmul_mx(
-                out=acc[i, h][:],
+                out=acc[part][:],
                 lhsT=wq[i, g][0][:].bitcast(FP8X4),
                 lhsT_scale=wq[i, g][1][:],
-                rhs=xq[g, h][0].bitcast(FP8X4),
-                rhs_scale=xq[g, h][1],
+                rhs=x_codes[g][:, cols].bitcast(FP8X4),
+                rhs_scale=x_scales[g][:, cols],
                 start=(g == 0),
                 stop=(g == PASSES - 1),
             )
 
         quantize_w(0, 0)
-        product(0, 0, 0)
-        product(0, 0, 1)
-        quantize_x1(0)
+        for q in range(PARTS):
+            product(score, 0, 0, q, SP)
         quantize_w(0, 1)
-        product(0, 1, 0)
-        quantize_x1(1)
-        product(0, 1, 1)
-        quantize_w(1, 0)
-        product(1, 0, 0)
-        product(1, 0, 1)
+        for q in range(PARTS):
+            quantize_x1(q)
+            product(score, 0, 1, q, SP)
 
+        def value_pass(g):
+            quantize_w(1, g)
+            for h in range(HALVES):
+                product(value, 1, g, h, SH)
+
+        e = [keep.tile([P, PH, D, VP], F32, name="e%d" % h) for h in range(HALVES)]
         top = {}
-        for h in range(HALVES):
-            top[h] = keep.tile([P, VH], F32, name="top%d" % h)
+
+        def largest(q):
+            tag = "w_raw1_1" if q == 2 else "top%d" % q
+            top[q] = keep.tile([P, VP], F32, name="top%d" % q, align_bytes=64, tag=tag)
             nc.vector.tensor_reduce(
-                out=top[h][:], in_=acc[0, h][:].rearrange("p (d v) -> p v d", d=D), axis=AX.X, op=ALU.max
+                out=top[q][:], in_=score[q][:].rearrange("p (d v) -> p v d", d=D), axis=AX.X, op=ALU.max
             )
-            if h == 0:
-                quantize_w(1, 1)
-                product(1, 1, 0)
-                product(1, 1, 1)
-        terms = {}
-        for h in range(HALVES):
-            shifted = keep.tile([P, D, VH], F32, name="shifted%d" % h)
+
+        def exponential(q):
+            shifted = keep.tile([P, D, VP], F32, name="shifted%d" % q)
             nc.vector.tensor_tensor(
                 out=shifted[:],
-                in0=acc[0, h][:].rearrange("p (d v) -> p d v", d=D),
-                in1=top[h][:].unsqueeze(1).to_broadcast([P, D, VH]),
+                in0=score[q][:].rearrange("p (d v) -> p d v", d=D),
+                in1=top[q][:].unsqueeze(1).to_broadcast([P, D, VP]),
                 op=ALU.subtract,
             )
-            terms[h] = keep.tile([P, 2, SH], F32, name="terms%d" % h)
-            nc.scalar.activation(out=terms[h][:, 0, :], in_=shifted[:].rearrange("p d v -> p (d v)"), func=ACT.Exp)
+            nc.scalar.activation(out=e[q // PH][:, q % PH], in_=shifted[:], func=ACT.Exp)
+
+        value_pass(0)
+        largest(0)
+        largest(1)
+        exponential(0)
+        exponential(1)
+        value_pass(1)
+        largest(2)
+        largest(3)
+        exponential(2)
+        exponential(3)
+
+        den_other = keep.tile([P, HALVES, PH, VP], F32, name="den_other")
+        num = keep.tile([P, HALVES, PH, VP], F32, name="num")
+        eh = [keep.tile([P, PH, D, VP], F32, name="eh%d" % h) for h in range(HALVES)]
+
+        def sum_pieces(dst, src):
+            nc.vector.tensor_reduce(out=dst, in_=src[:].rearrange("p q d v -> p q v d"), axis=AX.X, op=ALU.add)
+
         for h in range(HALVES):
-            nc.vector.tensor_tensor(out=terms[h][:, 1, :], in0=acc[1, h][:], in1=terms[h][:, 0, :], op=ALU.mult)
-        pairs = {}
-        for h in range(HALVES):
-            pairs[h] = keep.tile([P, 2, 2 * VH], F32, name="pairs%d" % h)
+            sum_pieces(den_other[:, 1 - h], e[h])
             nc.vector.tensor_tensor(
-                out=pairs[h][:], in0=terms[h][:, :, : 2 * VH], in1=terms[h][:, :, 2 * VH :], op=ALU.add
+                out=eh[h][:].rearrange("p q d v -> p (q d v)"),
+                in0=value[h][:],
+                in1=e[h][:].rearrange("p q d v -> p (q d v)"),
+                op=ALU.mult,
             )
-        sums = {}
-        for h in range(HALVES):
-            sums[h] = keep.tile([P, 2, VH], F32, name="sums%d" % h)
-            nc.vector.tensor_tensor(out=sums[h][:], in0=pairs[h][:, :, :VH], in1=pairs[h][:, :, VH:], op=ALU.add)
+        den_flat = den_other[:].rearrange("p h q v -> p h (q v)")
         both = keep.tile([P, VH], F32, name="both")
-        nc.vector.tensor_tensor(out=both[:], in0=sums[0][:, 0, :], in1=sums[1][:, 0, :], op=ALU.mult)
-        cross = keep.tile([P, HALVES, VH], F32, name="cross")
-        nc.vector.tensor_tensor(out=cross[:, 0, :], in0=sums[0][:, 1, :], in1=sums[1][:, 0, :], op=ALU.mult)
+        nc.vector.tensor_tensor(out=both[:], in0=den_flat[:, 0], in1=den_flat[:, 1], op=ALU.mult)
+        sum_pieces(num[:, 0], eh[0])
         rec = keep.tile([P, VH], F32, name="rec")
         nc.vector.reciprocal(out=rec[:], in_=both[:])
-        nc.vector.tensor_tensor(out=cross[:, 1, :], in0=sums[1][:, 1, :], in1=sums[0][:, 0, :], op=ALU.mult)
-        res = keep.tile([P, HALVES, VH], F32, name="res")
+        sum_pieces(num[:, 1], eh[1])
+        inv = keep.tile([P, HALVES, VH], F32, name="inv")
         nc.vector.tensor_tensor(
-            out=res[:], in0=cross[:], in1=rec[:].unsqueeze(1).to_broadcast([P, HALVES, VH]), op=ALU.mult
+            out=inv[:], in0=den_flat, in1=rec[:].unsqueeze(1).to_broadcast([P, HALVES, VH]), op=ALU.mult
         )
-        nc.sync.dma_start(out=out, in_=res[:].rearrange("p h v -> p (h v)"))
+        res = keep.tile([P, V], F32, name="res")
+        nc.vector.tensor_tensor(
+            out=res[:],
+            in0=num[:].rearrange("p h q v -> p (h q v)"),
+            in1=inv[:].rearrange("p h v -> p (h v)"),
+            op=ALU.mult,
+        )
+        nc.sync.dma_start(out=out, in_=res[:])

@@ -123,7 +123,7 @@ def tile_picked_apool_none_e_kernel(tc, xT, w1, w2, offs, out):
             for h in range(HALVES):
                 product(value, 1, g, h, SH)
 
-        e = [keep.tile([P, PH, D, VP], F32, name="e%d" % h) for h in range(HALVES)]
+        e = [keep.tile([P, PH, VP, D], F32, name="e%d" % h) for h in range(HALVES)]
         top = {}
 
         def largest(q):
@@ -134,11 +134,11 @@ def tile_picked_apool_none_e_kernel(tc, xT, w1, w2, offs, out):
             )
 
         def exponential(q):
-            shifted = keep.tile([P, D, VP], F32, name="shifted%d" % q)
+            shifted = keep.tile([P, VP, D], F32, name="shifted%d" % q)
             nc.vector.tensor_tensor(
                 out=shifted[:],
-                in0=score[q][:].rearrange("p (d v) -> p d v", d=D),
-                in1=top[q][:].unsqueeze(1).to_broadcast([P, D, VP]),
+                in0=score[q][:].rearrange("p (d v) -> p v d", d=D),
+                in1=top[q][:].unsqueeze(2).to_broadcast([P, VP, D]),
                 op=ALU.subtract,
             )
             nc.scalar.activation(out=e[q // PH][:, q % PH], in_=shifted[:], func=ACT.Exp)
@@ -156,17 +156,17 @@ def tile_picked_apool_none_e_kernel(tc, xT, w1, w2, offs, out):
 
         den_other = keep.tile([P, HALVES, PH, VP], F32, name="den_other")
         num = keep.tile([P, HALVES, PH, VP], F32, name="num")
-        eh = [keep.tile([P, PH, D, VP], F32, name="eh%d" % h) for h in range(HALVES)]
+        eh = [keep.tile([P, PH, VP, D], F32, name="eh%d" % h) for h in range(HALVES)]
 
         def sum_pieces(dst, src):
-            nc.vector.tensor_reduce(out=dst, in_=src[:].rearrange("p q d v -> p q v d"), axis=AX.X, op=ALU.add)
+            nc.vector.tensor_reduce(out=dst, in_=src[:], axis=AX.X, op=ALU.add)
 
         for h in range(HALVES):
             sum_pieces(den_other[:, 1 - h], e[h])
             nc.vector.tensor_tensor(
-                out=eh[h][:].rearrange("p q d v -> p (q d v)"),
-                in0=value[h][:],
-                in1=e[h][:].rearrange("p q d v -> p (q d v)"),
+                out=eh[h][:],
+                in0=value[h][:].rearrange("p (q d v) -> p q v d", q=PH, d=D),
+                in1=e[h][:],
                 op=ALU.mult,
             )
         den_flat = den_other[:].rearrange("p h q v -> p h (q v)")

@@ -50,11 +50,6 @@ def tile_picked_apool_none_e_kernel(tc, xT, w1, w2, offs, out):
                 w_raw[i, g] = keep.tile([P, PACK, N], F32, name="w_raw%d_%d" % (i, g), align_bytes=64)
                 nc.sync.dma_start(out=w_raw[i, g][:], in_=w_rows[g])
 
-        warm_in = keep.tile([P, 1], F32, name="warm_in")
-        warm_out = keep.tile([P, 1], F32, name="warm_out")
-        nc.vector.memset(warm_in[:], 0.0)
-        nc.scalar.activation(out=warm_out[:], in_=warm_in[:], func=ACT.Exp)
-
         def gather(g):
             picked = keep.tile([P, S, PACK], BF16, name="picked%d" % g, align_bytes=64)
             by_entry = picked[:].rearrange("p (q d v) j -> p j d q v", q=PARTS, d=D)
@@ -98,7 +93,7 @@ def tile_picked_apool_none_e_kernel(tc, xT, w1, w2, offs, out):
         score = [psum.tile([P, SP], F32, name="score%d" % q) for q in range(PARTS)]
         value = [psum.tile([P, SH], F32, name="value%d" % h) for h in range(HALVES)]
 
-        def product(acc, i, g, part, width):
+        def product(acc, i, g, part, width, start):
             cols = slice(part * width, (part + 1) * width)
             nc.tensor.matmul_mx(
                 out=acc[part][:],
@@ -106,24 +101,24 @@ def tile_picked_apool_none_e_kernel(tc, xT, w1, w2, offs, out):
                 lhsT_scale=wq[i, g][1][:],
                 rhs=x_codes[g][:, cols].bitcast(FP8X4),
                 rhs_scale=x_scales[g][:, cols],
-                start=(g == 0),
-                stop=(g == PASSES - 1),
+                start=start,
+                stop=not start,
             )
 
         quantize_w(0, 0)
         for q in range(PARTS):
-            product(score, 0, 0, q, SP)
+            product(score, 0, 0, q, SP, True)
         quantize_w(0, 1)
         for q in range(PARTS):
             quantize_x1(q)
-            product(score, 0, 1, q, SP)
+            product(score, 0, 1, q, SP, False)
 
         def value_pass(g):
             quantize_w(1, g)
             for h in range(HALVES):
-                product(value, 1, g, h, SH)
+                product(value, 1, g, h, SH, g == 0)
 
-        e = [keep.tile([P, PH, VP, D], F32, name="e%d" % h) for h in range(HALVES)]
+        e = [keep.tile([P, D, PH, VP], F32, name="e0"), keep.tile([P, PH, VP, D], F32, name="e1")]
         top = {}
 
         def largest(q):
@@ -134,14 +129,18 @@ def tile_picked_apool_none_e_kernel(tc, xT, w1, w2, offs, out):
             )
 
         def exponential(q):
-            shifted = keep.tile([P, VP, D], F32, name="shifted%d" % q)
-            nc.vector.tensor_tensor(
-                out=shifted[:],
-                in0=score[q][:].rearrange("p (d v) -> p v d", d=D),
-                in1=top[q][:].unsqueeze(2).to_broadcast([P, VP, D]),
-                op=ALU.subtract,
-            )
-            nc.scalar.activation(out=e[q // PH][:, q % PH], in_=shifted[:], func=ACT.Exp)
+            if q < PH:
+                shifted = keep.tile([P, D, VP], F32, name="shifted%d" % q)
+                scores = score[q][:].rearrange("p (d v) -> p d v", d=D)
+                tops = top[q][:].unsqueeze(1).to_broadcast([P, D, VP])
+                dst = e[0][:, :, q]
+            else:
+                shifted = keep.tile([P, VP, D], F32, name="shifted%d" % q)
+                scores = score[q][:].rearrange("p (d v) -> p v d", d=D)
+                tops = top[q][:].unsqueeze(2).to_broadcast([P, VP, D])
+                dst = e[1][:, q - PH]
+            nc.vector.tensor_tensor(out=shifted[:], in0=scores, in1=tops, op=ALU.subtract)
+            nc.scalar.activation(out=dst, in_=shifted[:], func=ACT.Exp)
 
         value_pass(0)
         largest(0)
@@ -154,37 +153,38 @@ def tile_picked_apool_none_e_kernel(tc, xT, w1, w2, offs, out):
         exponential(2)
         exponential(3)
 
-        den_other = keep.tile([P, HALVES, PH, VP], F32, name="den_other")
-        num = keep.tile([P, HALVES, PH, VP], F32, name="num")
-        eh = [keep.tile([P, PH, VP, D], F32, name="eh%d" % h) for h in range(HALVES)]
+        den_other = keep.tile([P, HALVES, VH], F32, name="den_other")
+        num = keep.tile([P, HALVES, VH], F32, name="num")
+        eh0 = keep.tile([P, D, PH, VP], F32, name="eh0")
+        eh1 = keep.tile([P, PH, VP, D], F32, name="eh1")
+
+        def fold(dst, src, name):
+            flat = src[:].rearrange("p d q v -> p d (q v)")
+            two = keep.tile([P, 2, VH], F32, name=name)
+            nc.gpsimd.tensor_tensor(out=two[:], in0=flat[:, 0:2], in1=flat[:, 2:4], op=ALU.add)
+            nc.gpsimd.tensor_tensor(out=dst, in0=two[:, 0], in1=two[:, 1], op=ALU.add)
 
         def sum_pieces(dst, src):
-            nc.vector.tensor_reduce(out=dst, in_=src[:], axis=AX.X, op=ALU.add)
+            nc.vector.tensor_reduce(out=dst, in_=src[:].rearrange("p q v d -> p (q v) d"), axis=AX.X, op=ALU.add)
 
-        for h in range(HALVES):
-            sum_pieces(den_other[:, 1 - h], e[h])
-            nc.vector.tensor_tensor(
-                out=eh[h][:],
-                in0=value[h][:].rearrange("p (q d v) -> p q v d", q=PH, d=D),
-                in1=e[h][:],
-                op=ALU.mult,
-            )
-        den_flat = den_other[:].rearrange("p h q v -> p h (q v)")
+        fold(den_other[:, 1], e[0], "den_two")
+        nc.vector.tensor_tensor(
+            out=eh0[:], in0=value[0][:].rearrange("p (q d v) -> p d q v", q=PH, d=D), in1=e[0][:], op=ALU.mult
+        )
+        fold(num[:, 0], eh0, "num_two")
+        sum_pieces(den_other[:, 0], e[1])
+        nc.vector.tensor_tensor(
+            out=eh1[:], in0=value[1][:].rearrange("p (q d v) -> p q v d", q=PH, d=D), in1=e[1][:], op=ALU.mult
+        )
         both = keep.tile([P, VH], F32, name="both")
-        nc.vector.tensor_tensor(out=both[:], in0=den_flat[:, 0], in1=den_flat[:, 1], op=ALU.mult)
-        sum_pieces(num[:, 0], eh[0])
+        nc.vector.tensor_reduce(out=both[:], in_=den_other[:].rearrange("p h v -> p v h"), axis=AX.X, op=ALU.mult)
+        sum_pieces(num[:, 1], eh1)
         rec = keep.tile([P, VH], F32, name="rec")
         nc.vector.reciprocal(out=rec[:], in_=both[:])
-        sum_pieces(num[:, 1], eh[1])
-        inv = keep.tile([P, HALVES, VH], F32, name="inv")
+        cross = keep.tile([P, HALVES, VH], F32, name="cross")
+        nc.vector.tensor_tensor(out=cross[:], in0=num[:], in1=den_other[:], op=ALU.mult)
+        res = keep.tile([P, HALVES, VH], F32, name="res")
         nc.vector.tensor_tensor(
-            out=inv[:], in0=den_flat, in1=rec[:].unsqueeze(1).to_broadcast([P, HALVES, VH]), op=ALU.mult
+            out=res[:], in0=cross[:], in1=rec[:].unsqueeze(1).to_broadcast([P, HALVES, VH]), op=ALU.mult
         )
-        res = keep.tile([P, V], F32, name="res")
-        nc.vector.tensor_tensor(
-            out=res[:],
-            in0=num[:].rearrange("p h q v -> p (h q v)"),
-            in1=inv[:].rearrange("p h v -> p (h v)"),
-            op=ALU.mult,
-        )
-        nc.sync.dma_start(out=out, in_=res[:])
+        nc.sync.dma_start(out=out, in_=res[:].rearrange("p h v -> p (h v)"))

@@ -158,33 +158,49 @@ def tile_picked_apool_none_e_kernel(tc, xT, w1, w2, offs, out):
         eh0 = keep.tile([P, D, PH, VP], F32, name="eh0")
         eh1 = keep.tile([P, PH, VP, D], F32, name="eh1")
 
-        def fold(dst, src, name):
+        def fold_four(engine, src, name):
             flat = src[:].rearrange("p d q v -> p d (q v)")
             two = keep.tile([P, 2, VH], F32, name=name)
-            nc.gpsimd.tensor_tensor(out=two[:], in0=flat[:, 0:2], in1=flat[:, 2:4], op=ALU.add)
-            nc.gpsimd.tensor_tensor(out=dst, in0=two[:, 0], in1=two[:, 1], op=ALU.add)
+            engine.tensor_tensor(out=two[:], in0=flat[:, 0:2], in1=flat[:, 2:4], op=ALU.add)
+            return two
+
+        def fold_two(engine, dst, two):
+            engine.tensor_tensor(out=dst, in0=two[:, 0], in1=two[:, 1], op=ALU.add)
 
         def sum_pieces(dst, src):
             nc.vector.tensor_reduce(out=dst, in_=src[:].rearrange("p q v d -> p (q v) d"), axis=AX.X, op=ALU.add)
 
-        fold(den_other[:, 1], e[0], "den_two")
+        nc.vector.tensor_reduce(
+            out=den_other[:, 1], in_=e[0][:].rearrange("p d q v -> p (q v) d"), axis=AX.X, op=ALU.add
+        )
         nc.vector.tensor_tensor(
             out=eh0[:], in0=value[0][:].rearrange("p (q d v) -> p d q v", q=PH, d=D), in1=e[0][:], op=ALU.mult
         )
-        fold(num[:, 0], eh0, "num_two")
-        sum_pieces(den_other[:, 0], e[1])
-        nc.vector.tensor_tensor(
-            out=eh1[:], in0=value[1][:].rearrange("p (q d v) -> p q v d", q=PH, d=D), in1=e[1][:], op=ALU.mult
-        )
+        fold_two(nc.gpsimd, num[:, 0], fold_four(nc.gpsimd, eh0, "num_two"))
+        def weigh_late(q):
+            cols = slice(q * SP, (q + 1) * SP)
+            nc.vector.tensor_tensor(
+                out=eh1[:, q], in0=value[1][:, cols].rearrange("p (d v) -> p v d", d=D), in1=e[1][:, q], op=ALU.mult
+            )
+
+        def den_late(q):
+            nc.vector.tensor_reduce(
+                out=den_other[:, 0, q * VP : (q + 1) * VP], in_=e[1][:, q], axis=AX.X, op=ALU.add
+            )
+
+        weigh_late(0)
+        den_late(0)
+        den_late(1)
+        weigh_late(1)
         both = keep.tile([P, VH], F32, name="both")
         nc.vector.tensor_reduce(out=both[:], in_=den_other[:].rearrange("p h v -> p v h"), axis=AX.X, op=ALU.mult)
         sum_pieces(num[:, 1], eh1)
         rec = keep.tile([P, VH], F32, name="rec")
         nc.vector.reciprocal(out=rec[:], in_=both[:])
-        cross = keep.tile([P, HALVES, VH], F32, name="cross")
-        nc.vector.tensor_tensor(out=cross[:], in0=num[:], in1=den_other[:], op=ALU.mult)
+        cross = [keep.tile([P, VH], F32, name="cross%d" % h) for h in range(HALVES)]
         res = keep.tile([P, HALVES, VH], F32, name="res")
-        nc.vector.tensor_tensor(
-            out=res[:], in0=cross[:], in1=rec[:].unsqueeze(1).to_broadcast([P, HALVES, VH]), op=ALU.mult
-        )
+        nc.gpsimd.tensor_tensor(out=cross[0][:], in0=num[:, 0], in1=den_other[:, 0], op=ALU.mult)
+        nc.vector.tensor_tensor(out=cross[1][:], in0=num[:, 1], in1=den_other[:, 1], op=ALU.mult)
+        for h in range(HALVES):
+            nc.vector.tensor_tensor(out=res[:, h], in0=cross[h][:], in1=rec[:], op=ALU.mult)
         nc.sync.dma_start(out=out, in_=res[:].rearrange("p h v -> p (h v)"))

@@ -197,10 +197,10 @@ def tile_picked_apool_none_e_kernel(tc, xT, w1, w2, offs, out):
         sum_pieces(num[:, 1], eh1)
         rec = keep.tile([P, VH], F32, name="rec")
         nc.vector.reciprocal(out=rec[:], in_=both[:])
-        cross = [keep.tile([P, VH], F32, name="cross%d" % h) for h in range(HALVES)]
+        cross = keep.tile([P, HALVES, VH], F32, name="cross")
+        nc.vector.tensor_tensor(out=cross[:], in0=num[:], in1=den_other[:], op=ALU.mult)
         res = keep.tile([P, HALVES, VH], F32, name="res")
-        nc.gpsimd.tensor_tensor(out=cross[0][:], in0=num[:, 0], in1=den_other[:, 0], op=ALU.mult)
-        nc.vector.tensor_tensor(out=cross[1][:], in0=num[:, 1], in1=den_other[:, 1], op=ALU.mult)
-        for h in range(HALVES):
-            nc.vector.tensor_tensor(out=res[:, h], in0=cross[h][:], in1=rec[:], op=ALU.mult)
+        nc.vector.tensor_tensor(
+            out=res[:], in0=cross[:], in1=rec[:].unsqueeze(1).to_broadcast([P, HALVES, VH]), op=ALU.mult
+        )
         nc.sync.dma_start(out=out, in_=res[:].rearrange("p h v -> p (h v)"))

@@ -106,12 +106,14 @@ def tile_picked_apool_none_e_kernel(tc, xT, w1, w2, offs, out):
             )
 
         quantize_w(0, 0)
-        for q in range(PARTS):
+        for q in range(PH):
             product(score, 0, 0, q, SP, True)
         quantize_w(0, 1)
         for q in range(PARTS):
             quantize_x1(q)
-            product(score, 0, 1, q, SP, False)
+            product(score, 0, 1, q, SP, q >= PH)
+            if q >= PH:
+                product(score, 0, 0, q, SP, False)
 
         def value_pass(g):
             quantize_w(1, g)

@@ -117,15 +117,16 @@ def tile_picked_apool_none_e_kernel(tc, xT, w1, w2, offs, out):
 
         def value_pass(g):
             quantize_w(1, g)
-            for h in range(HALVES):
-                product(value, 1, g, h, SH, g == 0)
+            product(value, 1, g, 0, SH, g == 0)
+            if g == 1:
+                product(value, 1, 1, 1, SH, True)
+                product(value, 1, 0, 1, SH, False)
 
         e = [keep.tile([P, D, PH, VP], F32, name="e0"), keep.tile([P, PH, VP, D], F32, name="e1")]
         top = {}
 
         def largest(q):
-            tag = "w_raw1_1" if q == 2 else "top%d" % q
-            top[q] = keep.tile([P, VP], F32, name="top%d" % q, align_bytes=64, tag=tag)
+            top[q] = keep.tile([P, VP], F32, name="top%d" % q, align_bytes=64)
             nc.vector.tensor_reduce(
                 out=top[q][:], in_=score[q][:].rearrange("p (d v) -> p v d", d=D), axis=AX.X, op=ALU.max
             )
@@ -169,8 +170,8 @@ def tile_picked_apool_none_e_kernel(tc, xT, w1, w2, offs, out):
         def fold_two(engine, dst, two):
             engine.tensor_tensor(out=dst, in0=two[:, 0], in1=two[:, 1], op=ALU.add)
 
-        def sum_pieces(dst, src):
-            nc.vector.tensor_reduce(out=dst, in_=src[:].rearrange("p q v d -> p (q v) d"), axis=AX.X, op=ALU.add)
+        def num_late(q):
+            nc.vector.tensor_reduce(out=num[:, 1, q * VP : (q + 1) * VP], in_=eh1[:, q], axis=AX.X, op=ALU.add)
 
         nc.vector.tensor_reduce(
             out=den_other[:, 1], in_=e[0][:].rearrange("p d q v -> p (q v) d"), axis=AX.X, op=ALU.add
@@ -190,19 +191,20 @@ def tile_picked_apool_none_e_kernel(tc, xT, w1, w2, offs, out):
                 out=den_other[:, 0, q * VP : (q + 1) * VP], in_=e[1][:, q], axis=AX.X, op=ALU.add
             )
 
-        weigh_late(0)
         den_late(0)
         den_late(1)
+        weigh_late(0)
         weigh_late(1)
         both = keep.tile([P, VH], F32, name="both")
         nc.vector.tensor_reduce(out=both[:], in_=den_other[:].rearrange("p h v -> p v h"), axis=AX.X, op=ALU.mult)
-        sum_pieces(num[:, 1], eh1)
+        num_late(0)
+        num_late(1)
         rec = keep.tile([P, VH], F32, name="rec")
         nc.vector.reciprocal(out=rec[:], in_=both[:])
         cross = keep.tile([P, HALVES, VH], F32, name="cross")
-        nc.vector.tensor_tensor(out=cross[:], in0=num[:], in1=den_other[:], op=ALU.mult)
         res = keep.tile([P, HALVES, VH], F32, name="res")
-        nc.vector.tensor_tensor(
-            out=res[:], in0=cross[:], in1=rec[:].unsqueeze(1).to_broadcast([P, HALVES, VH]), op=ALU.mult
-        )
+        for h in (1, 0):
+            nc.vector.tensor_tensor(out=cross[:, h], in0=num[:, h], in1=den_other[:, h], op=ALU.mult)
+        for h in (1, 0):
+            nc.vector.tensor_tensor(out=res[:, h], in0=cross[:, h], in1=rec[:], op=ALU.mult)
         nc.sync.dma_start(out=out, in_=res[:].rearrange("p h v -> p (h v)"))

@@ -26,6 +26,9 @@ HALVES = 2
 PH = PARTS // HALVES
 VH = V // HALVES
 SH = S // HALVES
+LIST_GROUP = 16
+RUN = 4
+SCORE_W, VALUE_W = 0, 1
 
 
 def tile_picked_apool_none_e_kernel(tc, xT, w1, w2, offs, out):
@@ -34,7 +37,7 @@ def tile_picked_apool_none_e_kernel(tc, xT, w1, w2, offs, out):
         keep = ctx.enter_context(tc.tile_pool(name="keep", bufs=1))
         psum = ctx.enter_context(tc.psum_pool(name="psum", bufs=1))
 
-        offsets = keep.tile([P, S // 16], U16, name="offsets")
+        offsets = keep.tile([P, S // LIST_GROUP], U16, name="offsets")
         x_rows = xT.rearrange("(g p j) t -> g j p t", g=PASSES, j=PACK)
         planes = {}
         for g in range(PASSES):
@@ -52,7 +55,7 @@ def tile_picked_apool_none_e_kernel(tc, xT, w1, w2, offs, out):
 
         def gather(g):
             picked = keep.tile([P, S, PACK], BF16, name="picked%d" % g, align_bytes=64)
-            by_entry = picked[:].rearrange("p (q d v) j -> p j d q v", q=PARTS, d=D)
+            by_entry = picked[:].rearrange("p (q d u) j -> p j d q u", q=PARTS, d=D)
             for j in range(PACK):
                 nc.vector.tensor_copy(by_entry[:, j], planes[g, j][:].indirect(offsets[:]))
             return picked[:].rearrange("p s j -> p (s j)")
@@ -60,8 +63,8 @@ def tile_picked_apool_none_e_kernel(tc, xT, w1, w2, offs, out):
         def round_w(i, g):
             grouped = keep.tile([P, N, PACK], BF16, name="w_bf%d_%d" % (i, g), align_bytes=64)
             nc.scalar.copy(
-                out=grouped[:].rearrange("p (c i) j -> p c j i", i=4),
-                in_=w_raw[i, g][:].rearrange("p j (c i) -> p c j i", i=4),
+                out=grouped[:].rearrange("p (c r) j -> p c j r", r=RUN),
+                in_=w_raw[i, g][:].rearrange("p j (c r) -> p c j r", r=RUN),
             )
             return grouped[:].rearrange("p n j -> p (n j)")
 
@@ -71,10 +74,10 @@ def tile_picked_apool_none_e_kernel(tc, xT, w1, w2, offs, out):
         x_scales[0] = keep.tile([P, S], U8, name="x_scales0", align_bytes=64)
         nc.vector.quantize_mx(out=x_codes[0][:].bitcast(FP8X4), scales=x_scales[0][:], in_=picked0)
         picked1 = gather(1)
-        w_bf = {(i, g): round_w(i, g) for i in range(2) for g in range(PASSES)}
+        w_bf = {(i, g): round_w(i, g) for i in (SCORE_W, VALUE_W) for g in range(PASSES)}
         x_codes[1] = keep.tile([P, S], U32, name="x_codes1", align_bytes=64, tag="w_raw0_1")
         x_scales[1] = keep.tile([P, S], U8, name="x_scales1", align_bytes=64)
-        wq = {}
+        w_mx = {}
 
         def quantize_x1(q):
             cols = slice(q * SP, (q + 1) * SP)
@@ -88,69 +91,64 @@ def tile_picked_apool_none_e_kernel(tc, xT, w1, w2, offs, out):
             codes = keep.tile([P, N], U32, name="w_codes%d_%d" % (i, g), align_bytes=64)
             scales = keep.tile([P, N], U8, name="w_scales%d_%d" % (i, g), align_bytes=64)
             nc.vector.quantize_mx(out=codes[:].bitcast(FP8X4), scales=scales[:], in_=w_bf[i, g])
-            wq[i, g] = (codes, scales)
+            w_mx[i, g] = (codes, scales)
 
         score = [psum.tile([P, SP], F32, name="score%d" % q) for q in range(PARTS)]
         value = [psum.tile([P, SH], F32, name="value%d" % h) for h in range(HALVES)]
 
-        def product(acc, i, g, part, width, start):
-            cols = slice(part * width, (part + 1) * width)
+        def product(bank, i, g, first_col, opens):
+            cols = slice(first_col, first_col + bank.shape[1])
             nc.tensor.matmul_mx(
-                out=acc[part][:],
-                lhsT=wq[i, g][0][:].bitcast(FP8X4),
-                lhsT_scale=wq[i, g][1][:],
+                out=bank[:],
+                lhsT=w_mx[i, g][0][:].bitcast(FP8X4),
+                lhsT_scale=w_mx[i, g][1][:],
                 rhs=x_codes[g][:, cols].bitcast(FP8X4),
                 rhs_scale=x_scales[g][:, cols],
-                start=start,
-                stop=not start,
+                start=opens,
+                stop=not opens,
             )
 
-        quantize_w(0, 0)
+        quantize_w(SCORE_W, 0)
         for q in range(PH):
-            product(score, 0, 0, q, SP, True)
-        quantize_w(0, 1)
+            product(score[q], SCORE_W, 0, q * SP, True)
+        quantize_w(SCORE_W, 1)
         for q in range(PARTS):
             quantize_x1(q)
-            product(score, 0, 1, q, SP, q >= PH)
-            if q >= PH:
-                product(score, 0, 0, q, SP, False)
+            if q < PH:
+                product(score[q], SCORE_W, 1, q * SP, False)
+            else:
+                product(score[q], SCORE_W, 1, q * SP, True)
+                product(score[q], SCORE_W, 0, q * SP, False)
 
-        def value_pass(g):
-            quantize_w(1, g)
-            product(value, 1, g, 0, SH, g == 0)
-            if g == 1:
-                product(value, 1, 1, 1, SH, True)
-                product(value, 1, 0, 1, SH, False)
-
-        e = [keep.tile([P, D, PH, VP], F32, name="e0"), keep.tile([P, PH, VP, D], F32, name="e1")]
+        e = [keep.tile([P, PH, VP, D], F32, name="e%d" % h) for h in range(HALVES)]
         top = {}
 
         def largest(q):
             top[q] = keep.tile([P, VP], F32, name="top%d" % q, align_bytes=64)
             nc.vector.tensor_reduce(
-                out=top[q][:], in_=score[q][:].rearrange("p (d v) -> p v d", d=D), axis=AX.X, op=ALU.max
+                out=top[q][:], in_=score[q][:].rearrange("p (d u) -> p u d", d=D), axis=AX.X, op=ALU.max
             )
 
         def exponential(q):
-            if q < PH:
-                shifted = keep.tile([P, D, VP], F32, name="shifted%d" % q)
-                scores = score[q][:].rearrange("p (d v) -> p d v", d=D)
-                tops = top[q][:].unsqueeze(1).to_broadcast([P, D, VP])
-                dst = e[0][:, :, q]
-            else:
-                shifted = keep.tile([P, VP, D], F32, name="shifted%d" % q)
-                scores = score[q][:].rearrange("p (d v) -> p v d", d=D)
-                tops = top[q][:].unsqueeze(2).to_broadcast([P, VP, D])
-                dst = e[1][:, q - PH]
-            nc.vector.tensor_tensor(out=shifted[:], in0=scores, in1=tops, op=ALU.subtract)
-            nc.scalar.activation(out=dst, in_=shifted[:], func=ACT.Exp)
+            shifted = keep.tile([P, VP, D], F32, name="shifted%d" % q)
+            nc.vector.tensor_tensor(
+                out=shifted[:],
+                in0=score[q][:].rearrange("p (d u) -> p u d", d=D),
+                in1=top[q][:].unsqueeze(2).to_broadcast([P, VP, D]),
+                op=ALU.subtract,
+            )
+            nc.scalar.activation(out=e[q // PH][:, q % PH], in_=shifted[:], func=ACT.Exp)
 
-        value_pass(0)
+        quantize_w(VALUE_W, 0)
+        product(value[0], VALUE_W, 0, 0, True)
         largest(0)
         largest(1)
         exponential(0)
         exponential(1)
-        value_pass(1)
+        quantize_w(VALUE_W, 1)
+        product(value[0], VALUE_W, 1, 0, False)
+        product(value[1], VALUE_W, 1, SH, True)
+        product(value[1], VALUE_W, 0, SH, False)
         largest(2)
         largest(3)
         exponential(2)
@@ -158,53 +156,48 @@ def tile_picked_apool_none_e_kernel(tc, xT, w1, w2, offs, out):
 
         den_other = keep.tile([P, HALVES, VH], F32, name="den_other")
         num = keep.tile([P, HALVES, VH], F32, name="num")
-        eh0 = keep.tile([P, D, PH, VP], F32, name="eh0")
-        eh1 = keep.tile([P, PH, VP, D], F32, name="eh1")
-
-        def fold_four(engine, src, name):
-            flat = src[:].rearrange("p d q v -> p d (q v)")
-            two = keep.tile([P, 2, VH], F32, name=name)
-            engine.tensor_tensor(out=two[:], in0=flat[:, 0:2], in1=flat[:, 2:4], op=ALU.add)
-            return two
-
-        def fold_two(engine, dst, two):
-            engine.tensor_tensor(out=dst, in0=two[:, 0], in1=two[:, 1], op=ALU.add)
-
-        def num_late(q):
-            nc.vector.tensor_reduce(out=num[:, 1, q * VP : (q + 1) * VP], in_=eh1[:, q], axis=AX.X, op=ALU.add)
+        weighted = [keep.tile([P, PH, VP, D], F32, name="weighted%d" % h) for h in range(HALVES)]
 
         nc.vector.tensor_reduce(
-            out=den_other[:, 1], in_=e[0][:].rearrange("p d q v -> p (q v) d"), axis=AX.X, op=ALU.add
+            out=den_other[:, 1], in_=e[0][:].rearrange("p q u d -> p (q u) d"), axis=AX.X, op=ALU.add
         )
         nc.vector.tensor_tensor(
-            out=eh0[:], in0=value[0][:].rearrange("p (q d v) -> p d q v", q=PH, d=D), in1=e[0][:], op=ALU.mult
+            out=weighted[0][:],
+            in0=value[0][:].rearrange("p (q d u) -> p q u d", q=PH, d=D),
+            in1=e[0][:],
+            op=ALU.mult,
         )
-        fold_two(nc.gpsimd, num[:, 0], fold_four(nc.gpsimd, eh0, "num_two"))
-        def weigh_late(q):
-            cols = slice(q * SP, (q + 1) * SP)
-            nc.vector.tensor_tensor(
-                out=eh1[:, q], in0=value[1][:, cols].rearrange("p (d v) -> p v d", d=D), in1=e[1][:, q], op=ALU.mult
-            )
+        by_place = weighted[0][:].rearrange("p q u d -> p (q u) d")
+        pair_sums = keep.tile([P, VH, 2], F32, name="pair_sums")
+        nc.gpsimd.tensor_tensor(out=pair_sums[:], in0=by_place[:, :, 0:2], in1=by_place[:, :, 2:4], op=ALU.add)
+        nc.gpsimd.tensor_tensor(out=num[:, 0], in0=pair_sums[:, :, 0], in1=pair_sums[:, :, 1], op=ALU.add)
 
-        def den_late(q):
+        for q in range(PH):
             nc.vector.tensor_reduce(
                 out=den_other[:, 0, q * VP : (q + 1) * VP], in_=e[1][:, q], axis=AX.X, op=ALU.add
             )
-
-        den_late(0)
-        den_late(1)
-        weigh_late(0)
-        weigh_late(1)
-        both = keep.tile([P, VH], F32, name="both")
-        nc.vector.tensor_reduce(out=both[:], in_=den_other[:].rearrange("p h v -> p v h"), axis=AX.X, op=ALU.mult)
-        num_late(0)
-        num_late(1)
+        for q in range(PH):
+            nc.vector.tensor_tensor(
+                out=weighted[1][:, q],
+                in0=value[1][:, q * SP : (q + 1) * SP].rearrange("p (d u) -> p u d", d=D),
+                in1=e[1][:, q],
+                op=ALU.mult,
+            )
+        den_both = keep.tile([P, VH], F32, name="den_both")
+        nc.vector.tensor_reduce(
+            out=den_both[:], in_=den_other[:].rearrange("p h v -> p v h"), axis=AX.X, op=ALU.mult
+        )
+        for q in range(PH):
+            nc.vector.tensor_reduce(
+                out=num[:, 1, q * VP : (q + 1) * VP], in_=weighted[1][:, q], axis=AX.X, op=ALU.add
+            )
         rec = keep.tile([P, VH], F32, name="rec")
-        nc.vector.reciprocal(out=rec[:], in_=both[:])
+        nc.vector.reciprocal(out=rec[:], in_=den_both[:])
+
         cross = keep.tile([P, HALVES, VH], F32, name="cross")
         res = keep.tile([P, HALVES, VH], F32, name="res")
-        for h in (1, 0):
+        for h in reversed(range(HALVES)):
             nc.vector.tensor_tensor(out=cross[:, h], in0=num[:, h], in1=den_other[:, h], op=ALU.mult)
-        for h in (1, 0):
+        for h in reversed(range(HALVES)):
             nc.vector.tensor_tensor(out=res[:, h], in0=cross[:, h], in1=rec[:], op=ALU.mult)
         nc.sync.dma_start(out=out, in_=res[:].rearrange("p h v -> p (h v)"))

@@ -28,6 +28,7 @@ VH = V // HALVES
 SH = S // HALVES
 LIST_GROUP = 16
 RUN = 4
+LOADS = ((0, 0, 2), (0, 2, 2), (1, 0, 2), (1, 2, 1), (1, 3, 1))
 SCORE_W, VALUE_W = 0, 1
 
 
@@ -38,14 +39,15 @@ def tile_picked_apool_none_e_kernel(tc, xT, w1, w2, offs, out):
         psum = ctx.enter_context(tc.psum_pool(name="psum", bufs=1))
 
         offsets = keep.tile([P, S // LIST_GROUP], U16, name="offsets")
-        x_rows = xT.rearrange("(g p j) t -> g j p t", g=PASSES, j=PACK)
+        x_rows = xT.rearrange("(g p j) t -> g p j t", g=PASSES, j=PACK)
         planes = {}
-        for g in range(PASSES):
-            for j in range(PACK):
-                planes[g, j] = keep.tile([P, T], F32, name="plane%d_%d" % (g, j))
-                nc.sync.dma_start(out=planes[g, j][:], in_=x_rows[g, j])
-                if (g, j) == (0, 0):
-                    nc.sync.dma_start(offsets[:], offs)
+        for g, j0, n in LOADS:
+            loaded = keep.tile([P, n, T], F32, name="planes%d_%d" % (g, j0))
+            nc.sync.dma_start(out=loaded[:], in_=x_rows[g, :, j0 : j0 + n])
+            for j in range(j0, j0 + n):
+                planes[g, j] = loaded[:, j - j0]
+            if (g, j0) == (0, 0):
+                nc.sync.dma_start(offsets[:], offs)
         w_raw = {}
         for i, w in enumerate((w1, w2)):
             w_rows = w.rearrange("(g p j) n -> g p j n", g=PASSES, j=PACK)
@@ -53,12 +55,24 @@ def tile_picked_apool_none_e_kernel(tc, xT, w1, w2, offs, out):
                 w_raw[i, g] = keep.tile([P, PACK, N], F32, name="w_raw%d_%d" % (i, g), align_bytes=64)
                 nc.sync.dma_start(out=w_raw[i, g][:], in_=w_rows[g])
 
-        def gather(g):
-            picked = keep.tile([P, S, PACK], BF16, name="picked%d" % g, align_bytes=64)
-            by_entry = picked[:].rearrange("p (q d u) j -> p j d q u", q=PARTS, d=D)
-            for j in range(PACK):
-                nc.vector.tensor_copy(by_entry[:, j], planes[g, j][:].indirect(offsets[:]))
-            return picked[:].rearrange("p s j -> p (s j)")
+        piece_cols = V // LIST_GROUP
+        first_pieces = offsets[:, : (D - 1) * piece_cols]
+        last_piece = offsets[:, (D - 1) * piece_cols :]
+        picked, by_entry, rows = {}, {}, {}
+        for g in range(PASSES):
+            picked[g] = keep.tile([P, S, PACK], BF16, name="picked%d" % g, align_bytes=64)
+            by_entry[g] = picked[g][:].rearrange("p (q d u) j -> p d q u j", q=PARTS, d=D)
+            rows[g] = keep.tile([P, PACK, V], F32, name="rows%d" % g, align_bytes=64)
+
+        def gather_plane(g, j):
+            nc.vector.tensor_copy(by_entry[g][:, : D - 1, :, :, j], planes[g, j].indirect(first_pieces))
+            nc.scalar.activation(out=rows[g][:, j], in_=planes[g, j].indirect(last_piece), func=ACT.Copy)
+
+        def laid_in(g, j0, j1):
+            return (
+                by_entry[g][:, D - 1, :, :, j0:j1],
+                rows[g][:, j0:j1].rearrange("p j (q u) -> p q u j", q=PARTS),
+            )
 
         def round_w(i, g):
             grouped = keep.tile([P, N, PACK], BF16, name="w_bf%d_%d" % (i, g), align_bytes=64)
@@ -69,11 +83,20 @@ def tile_picked_apool_none_e_kernel(tc, xT, w1, w2, offs, out):
             return grouped[:].rearrange("p n j -> p (n j)")
 
         x_codes, x_scales = {}, {}
-        picked0 = gather(0)
+        for j in range(PACK):
+            gather_plane(0, j)
+        nc.scalar.copy(*laid_in(0, 0, PACK))
+        picked0 = picked[0][:].rearrange("p s j -> p (s j)")
         x_codes[0] = keep.tile([P, S], U32, name="x_codes0", align_bytes=64)
         x_scales[0] = keep.tile([P, S], U8, name="x_scales0", align_bytes=64)
         nc.vector.quantize_mx(out=x_codes[0][:].bitcast(FP8X4), scales=x_scales[0][:], in_=picked0)
-        picked1 = gather(1)
+        gather_plane(1, 0)
+        gather_plane(1, 1)
+        nc.scalar.copy(*laid_in(1, 0, 2))
+        for j in (2, 3):
+            gather_plane(1, j)
+            nc.gpsimd.tensor_copy(*laid_in(1, j, j + 1))
+        picked1 = picked[1][:].rearrange("p s j -> p (s j)")
         w_bf = {(i, g): round_w(i, g) for i in (SCORE_W, VALUE_W) for g in range(PASSES)}
         x_codes[1] = keep.tile([P, S], U32, name="x_codes1", align_bytes=64, tag="w_raw0_1")
         x_scales[1] = keep.tile([P, S], U8, name="x_scales1", align_bytes=64)
@@ -123,29 +146,36 @@ def tile_picked_apool_none_e_kernel(tc, xT, w1, w2, offs, out):
         e = [keep.tile([P, PH, VP, D], F32, name="e%d" % h) for h in range(HALVES)]
         top = {}
 
+        shifted = {}
+
         def largest(q):
-            top[q] = keep.tile([P, VP], F32, name="top%d" % q, align_bytes=64)
             nc.vector.tensor_reduce(
-                out=top[q][:], in_=score[q][:].rearrange("p (d u) -> p u d", d=D), axis=AX.X, op=ALU.max
+                out=top[q], in_=score[q][:].rearrange("p (d u) -> p u d", d=D), axis=AX.X, op=ALU.max
             )
 
         def exponential(q):
-            shifted = keep.tile([P, VP, D], F32, name="shifted%d" % q)
             nc.vector.tensor_tensor(
-                out=shifted[:],
+                out=shifted[q],
                 in0=score[q][:].rearrange("p (d u) -> p u d", d=D),
-                in1=top[q][:].unsqueeze(2).to_broadcast([P, VP, D]),
+                in1=top[q].unsqueeze(2).to_broadcast([P, VP, D]),
                 op=ALU.subtract,
             )
-            nc.scalar.activation(out=e[q // PH][:, q % PH], in_=shifted[:], func=ACT.Exp)
+            nc.scalar.activation(out=e[q // PH][:, q % PH], in_=shifted[q], func=ACT.Exp)
 
         quantize_w(VALUE_W, 0)
         product(value[0], VALUE_W, 0, 0, True)
+        tops0 = keep.tile([P, PH, VP], F32, name="tops0", align_bytes=64)
+        top[0], top[1] = tops0[:, 0], tops0[:, 1]
         largest(0)
         largest(1)
+        quantize_w(VALUE_W, 1)
+        shifted0 = keep.tile([P, PH, VP, D], F32, name="shifted0", align_bytes=64, tag="w_raw1_1")
+        shifted1 = keep.tile([P, PH, VP, D], F32, name="shifted1", align_bytes=64)
+        tops1 = keep.tile([P, PH, VP], F32, name="tops1", align_bytes=64, tag="w_bf1_1")
+        for q in range(PH):
+            shifted[q], shifted[PH + q], top[PH + q] = shifted0[:, q], shifted1[:, q], tops1[:, q]
         exponential(0)
         exponential(1)
-        quantize_w(VALUE_W, 1)
         product(value[0], VALUE_W, 1, 0, False)
         product(value[1], VALUE_W, 1, SH, True)
         product(value[1], VALUE_W, 0, SH, False)
@@ -195,7 +225,7 @@ def tile_picked_apool_none_e_kernel(tc, xT, w1, w2, offs, out):
         nc.vector.reciprocal(out=rec[:], in_=den_both[:])
 
         cross = keep.tile([P, HALVES, VH], F32, name="cross")
-        res = keep.tile([P, HALVES, VH], F32, name="res")
+        res = keep.tile([P, HALVES, VH], F32, name="res", tag="pair_sums")
         for h in reversed(range(HALVES)):
             nc.vector.tensor_tensor(out=cross[:, h], in0=num[:, h], in1=den_other[:, h], op=ALU.mult)
         for h in reversed(range(HALVES)):

@@ -28,7 +28,7 @@ VH = V // HALVES
 SH = S // HALVES
 LIST_GROUP = 16
 RUN = 4
-LOADS = ((0, 0, 2), (0, 2, 2), (1, 0, 2), (1, 2, 1), (1, 3, 1))
+LOADS = ((0, 0, 2), (0, 2, 2), (1, 0, 1), (1, 1, 1), (1, 2, 1), (1, 3, 1))
 SCORE_W, VALUE_W = 0, 1
 
 
@@ -42,7 +42,7 @@ def tile_picked_apool_none_e_kernel(tc, xT, w1, w2, offs, out):
         x_rows = xT.rearrange("(g p j) t -> g p j t", g=PASSES, j=PACK)
         planes = {}
         for g, j0, n in LOADS:
-            loaded = keep.tile([P, n, T], F32, name="planes%d_%d" % (g, j0))
+            loaded = keep.tile([P, n, T], F32, name="planes%d_%d" % (g, j0), align_bytes=64)
             nc.sync.dma_start(out=loaded[:], in_=x_rows[g, :, j0 : j0 + n])
             for j in range(j0, j0 + n):
                 planes[g, j] = loaded[:, j - j0]
@@ -55,24 +55,13 @@ def tile_picked_apool_none_e_kernel(tc, xT, w1, w2, offs, out):
                 w_raw[i, g] = keep.tile([P, PACK, N], F32, name="w_raw%d_%d" % (i, g), align_bytes=64)
                 nc.sync.dma_start(out=w_raw[i, g][:], in_=w_rows[g])
 
-        piece_cols = V // LIST_GROUP
-        first_pieces = offsets[:, : (D - 1) * piece_cols]
-        last_piece = offsets[:, (D - 1) * piece_cols :]
-        picked, by_entry, rows = {}, {}, {}
+        picked, by_entry = {}, {}
         for g in range(PASSES):
             picked[g] = keep.tile([P, S, PACK], BF16, name="picked%d" % g, align_bytes=64)
             by_entry[g] = picked[g][:].rearrange("p (q d u) j -> p d q u j", q=PARTS, d=D)
-            rows[g] = keep.tile([P, PACK, V], F32, name="rows%d" % g, align_bytes=64)
 
         def gather_plane(g, j):
-            nc.vector.tensor_copy(by_entry[g][:, : D - 1, :, :, j], planes[g, j].indirect(first_pieces))
-            nc.scalar.activation(out=rows[g][:, j], in_=planes[g, j].indirect(last_piece), func=ACT.Copy)
-
-        def laid_in(g, j0, j1):
-            return (
-                by_entry[g][:, D - 1, :, :, j0:j1],
-                rows[g][:, j0:j1].rearrange("p j (q u) -> p q u j", q=PARTS),
-            )
+            nc.vector.tensor_copy(by_entry[g][:, :, :, :, j], planes[g, j].indirect(offsets[:]))
 
         def round_w(i, g):
             grouped = keep.tile([P, N, PACK], BF16, name="w_bf%d_%d" % (i, g), align_bytes=64)
@@ -83,19 +72,22 @@ def tile_picked_apool_none_e_kernel(tc, xT, w1, w2, offs, out):
             return grouped[:].rearrange("p n j -> p (n j)")
 
         x_codes, x_scales = {}, {}
-        for j in range(PACK):
-            gather_plane(0, j)
-        nc.scalar.copy(*laid_in(0, 0, PACK))
+        gather_plane(0, 0)
+        gather_plane(0, 1)
+        rows = keep.tile([P, 2, S], F32, name="rows", align_bytes=64)
+        nc.vector.tensor_copy(rows[:, 0], planes[0, 2].indirect(offsets[:]))
+        nc.scalar.activation(out=rows[:, 1], in_=planes[0, 3].indirect(offsets[:]), func=ACT.Copy)
+        rows_by_entry = rows[:].rearrange("p j (d q u) -> p d q u j", d=D, q=PARTS)
+        for d in range(D):
+            nc.scalar.copy(by_entry[0][:, d, :, :, 2:4], rows_by_entry[:, d])
         picked0 = picked[0][:].rearrange("p s j -> p (s j)")
-        x_codes[0] = keep.tile([P, S], U32, name="x_codes0", align_bytes=64)
-        x_scales[0] = keep.tile([P, S], U8, name="x_scales0", align_bytes=64)
-        nc.vector.quantize_mx(out=x_codes[0][:].bitcast(FP8X4), scales=x_scales[0][:], in_=picked0)
         gather_plane(1, 0)
         gather_plane(1, 1)
-        nc.scalar.copy(*laid_in(1, 0, 2))
-        for j in (2, 3):
-            gather_plane(1, j)
-            nc.gpsimd.tensor_copy(*laid_in(1, j, j + 1))
+        x_codes[0] = keep.tile([P, S], U32, name="x_codes0", align_bytes=64, tag="planes1_1")
+        x_scales[0] = keep.tile([P, S], U8, name="x_scales0", align_bytes=64)
+        nc.vector.quantize_mx(out=x_codes[0][:].bitcast(FP8X4), scales=x_scales[0][:], in_=picked0)
+        gather_plane(1, 2)
+        gather_plane(1, 3)
         picked1 = picked[1][:].rearrange("p s j -> p (s j)")
         w_bf = {(i, g): round_w(i, g) for i in (SCORE_W, VALUE_W) for g in range(PASSES)}
         x_codes[1] = keep.tile([P, S], U32, name="x_codes1", align_bytes=64, tag="w_raw0_1")

@@ -28,7 +28,7 @@ VH = V // HALVES
 SH = S // HALVES
 LIST_GROUP = 16
 RUN = 4
-LOADS = ((0, 0, 2), (0, 2, 2), (1, 0, 1), (1, 1, 1), (1, 2, 1), (1, 3, 1))
+LOADS = ((0, 0, 2), (0, 2, 2), (1, 0, 2), (1, 2, 1), (1, 3, 1))
 SCORE_W, VALUE_W = 0, 1
 
 
@@ -63,34 +63,43 @@ def tile_picked_apool_none_e_kernel(tc, xT, w1, w2, offs, out):
         def gather_plane(g, j):
             nc.vector.tensor_copy(by_entry[g][:, :, :, :, j], planes[g, j].indirect(offsets[:]))
 
+        def gather_shared_pair(g):
+            rows = keep.tile([P, 2, S], F32, name="rows%d" % g, align_bytes=64)
+            nc.vector.tensor_copy(rows[:, 0], planes[g, 0].indirect(offsets[:]))
+            nc.scalar.activation(out=rows[:, 1], in_=planes[g, 1].indirect(offsets[:]), func=ACT.Copy)
+            rows_by_entry = rows[:].rearrange("p j (d q u) -> p d q u j", d=D, q=PARTS)
+            for d in range(D):
+                nc.scalar.copy(by_entry[g][:, d, :, :, 0:2], rows_by_entry[:, d])
+
+        zero = {}
+        for i in (SCORE_W, VALUE_W):
+            zero[i] = keep.tile([P, 1], F32, name="zero%d" % i, align_bytes=64)
+            nc.vector.memset(zero[i][:], 0.0)
+
         def round_w(i, g):
             grouped = keep.tile([P, N, PACK], BF16, name="w_bf%d_%d" % (i, g), align_bytes=64)
-            nc.scalar.copy(
+            nc.scalar.activation(
                 out=grouped[:].rearrange("p (c r) j -> p c j r", r=RUN),
                 in_=w_raw[i, g][:].rearrange("p j (c r) -> p c j r", r=RUN),
+                func=ACT.Identity,
+                bias=zero[i][:],
             )
             return grouped[:].rearrange("p n j -> p (n j)")
 
         x_codes, x_scales = {}, {}
-        gather_plane(0, 0)
-        gather_plane(0, 1)
-        rows = keep.tile([P, 2, S], F32, name="rows", align_bytes=64)
-        nc.vector.tensor_copy(rows[:, 0], planes[0, 2].indirect(offsets[:]))
-        nc.scalar.activation(out=rows[:, 1], in_=planes[0, 3].indirect(offsets[:]), func=ACT.Copy)
-        rows_by_entry = rows[:].rearrange("p j (d q u) -> p d q u j", d=D, q=PARTS)
-        for d in range(D):
-            nc.scalar.copy(by_entry[0][:, d, :, :, 2:4], rows_by_entry[:, d])
+        gather_shared_pair(0)
+        gather_plane(0, 2)
+        gather_plane(0, 3)
         picked0 = picked[0][:].rearrange("p s j -> p (s j)")
-        gather_plane(1, 0)
-        gather_plane(1, 1)
-        x_codes[0] = keep.tile([P, S], U32, name="x_codes0", align_bytes=64, tag="planes1_1")
+        x_codes[0] = keep.tile([P, S], U32, name="x_codes0", align_bytes=64)
         x_scales[0] = keep.tile([P, S], U8, name="x_scales0", align_bytes=64)
         nc.vector.quantize_mx(out=x_codes[0][:].bitcast(FP8X4), scales=x_scales[0][:], in_=picked0)
+        gather_shared_pair(1)
         gather_plane(1, 2)
         gather_plane(1, 3)
         picked1 = picked[1][:].rearrange("p s j -> p (s j)")
         w_bf = {(i, g): round_w(i, g) for i in (SCORE_W, VALUE_W) for g in range(PASSES)}
-        x_codes[1] = keep.tile([P, S], U32, name="x_codes1", align_bytes=64, tag="w_raw0_1")
+        x_codes[1] = keep.tile([P, S], U32, name="x_codes1", align_bytes=64, tag="zero0")
         x_scales[1] = keep.tile([P, S], U8, name="x_scales1", align_bytes=64)
         w_mx = {}
 
@@ -161,11 +170,11 @@ def tile_picked_apool_none_e_kernel(tc, xT, w1, w2, offs, out):
         largest(0)
         largest(1)
         quantize_w(VALUE_W, 1)
-        shifted0 = keep.tile([P, PH, VP, D], F32, name="shifted0", align_bytes=64, tag="w_raw1_1")
+        held = keep.tile([P, PH, D + 1, VP], F32, name="held", align_bytes=64, tag="zero1")
         shifted1 = keep.tile([P, PH, VP, D], F32, name="shifted1", align_bytes=64)
-        tops1 = keep.tile([P, PH, VP], F32, name="tops1", align_bytes=64, tag="w_bf1_1")
         for q in range(PH):
-            shifted[q], shifted[PH + q], top[PH + q] = shifted0[:, q], shifted1[:, q], tops1[:, q]
+            shifted[q] = held[:, q, :D].rearrange("p a b -> p (a b)").rearrange("p (u d) -> p u d", d=D)
+            shifted[PH + q], top[PH + q] = shifted1[:, q], held[:, q, D]
         exponential(0)
         exponential(1)
         product(value[0], VALUE_W, 1, 0, False)

@@ -28,7 +28,7 @@ VH = V // HALVES
 SH = S // HALVES
 LIST_GROUP = 16
 RUN = 4
-LOADS = ((0, 0, 2), (0, 2, 2), (1, 0, 2), (1, 2, 1), (1, 3, 1))
+LOADS = ((0, 0, 1), (0, 1, 1), (0, 2, 2), (1, 0, 2), (1, 2, 1), (1, 3, 1))
 SCORE_W, VALUE_W = 0, 1
 
 

from contextlib import ExitStack

import concourse.mybir as mybir

K, T, S, V, N = 1024, 2048, 512, 128, 128
FLOPS = 2 * 2 * K * N * S

F32 = mybir.dt.float32
BF16 = mybir.dt.bfloat16
U32 = mybir.dt.uint32
U16 = mybir.dt.uint16
U8 = mybir.dt.uint8
FP8X4 = mybir.dt.float8_e4m3fn_x4
ALU = mybir.AluOpType
ACT = mybir.ActivationFunctionType
AX = mybir.AxisListType

P = 128
PACK = 4
PASSES = K // (P * PACK)
D = S // V
PARTS = 4
VP = V // PARTS
SP = S // PARTS
HALVES = 2
PH = PARTS // HALVES
VH = V // HALVES
SH = S // HALVES
LIST_GROUP = 16
RUN = 4
LOADS = ((0, 0, 1), (0, 1, 1), (0, 2, 2), (1, 0, 2), (1, 2, 1), (1, 3, 1))
SCORE_W, VALUE_W = 0, 1


def tile_picked_apool_none_e_kernel(tc, xT, w1, w2, offs, out):
    nc = tc.nc
    with ExitStack() as ctx:
        keep = ctx.enter_context(tc.tile_pool(name="keep", bufs=1))
        psum = ctx.enter_context(tc.psum_pool(name="psum", bufs=1))

        offsets = keep.tile([P, S // LIST_GROUP], U16, name="offsets")
        x_rows = xT.rearrange("(g p j) t -> g p j t", g=PASSES, j=PACK)
        planes = {}
        for g, j0, n in LOADS:
            loaded = keep.tile([P, n, T], F32, name="planes%d_%d" % (g, j0), align_bytes=64)
            nc.sync.dma_start(out=loaded[:], in_=x_rows[g, :, j0 : j0 + n])
            for j in range(j0, j0 + n):
                planes[g, j] = loaded[:, j - j0]
            if (g, j0) == (0, 0):
                nc.sync.dma_start(offsets[:], offs)
        w_raw = {}
        for i, w in enumerate((w1, w2)):
            w_rows = w.rearrange("(g p j) n -> g p j n", g=PASSES, j=PACK)
            for g in range(PASSES):
                w_raw[i, g] = keep.tile([P, PACK, N], F32, name="w_raw%d_%d" % (i, g), align_bytes=64)
                nc.sync.dma_start(out=w_raw[i, g][:], in_=w_rows[g])

        picked, by_entry = {}, {}
        for g in range(PASSES):
            picked[g] = keep.tile([P, S, PACK], BF16, name="picked%d" % g, align_bytes=64)
            by_entry[g] = picked[g][:].rearrange("p (q d u) j -> p d q u j", q=PARTS, d=D)

        def gather_plane(g, j):
            nc.vector.tensor_copy(by_entry[g][:, :, :, :, j], planes[g, j].indirect(offsets[:]))

        def gather_shared_pair(g):
            rows = keep.tile([P, 2, S], F32, name="rows%d" % g, align_bytes=64)
            nc.vector.tensor_copy(rows[:, 0], planes[g, 0].indirect(offsets[:]))
            nc.scalar.activation(out=rows[:, 1], in_=planes[g, 1].indirect(offsets[:]), func=ACT.Copy)
            rows_by_entry = rows[:].rearrange("p j (d q u) -> p d q u j", d=D, q=PARTS)
            for d in range(D):
                nc.scalar.copy(by_entry[g][:, d, :, :, 0:2], rows_by_entry[:, d])

        zero = {}
        for i in (SCORE_W, VALUE_W):
            zero[i] = keep.tile([P, 1], F32, name="zero%d" % i, align_bytes=64)
            nc.vector.memset(zero[i][:], 0.0)

        def round_w(i, g):
            grouped = keep.tile([P, N, PACK], BF16, name="w_bf%d_%d" % (i, g), align_bytes=64)
            nc.scalar.activation(
                out=grouped[:].rearrange("p (c r) j -> p c j r", r=RUN),
                in_=w_raw[i, g][:].rearrange("p j (c r) -> p c j r", r=RUN),
                func=ACT.Identity,
                bias=zero[i][:],
            )
            return grouped[:].rearrange("p n j -> p (n j)")

        x_codes, x_scales = {}, {}
        gather_shared_pair(0)
        gather_plane(0, 2)
        gather_plane(0, 3)
        picked0 = picked[0][:].rearrange("p s j -> p (s j)")
        x_codes[0] = keep.tile([P, S], U32, name="x_codes0", align_bytes=64)
        x_scales[0] = keep.tile([P, S], U8, name="x_scales0", align_bytes=64)
        nc.vector.quantize_mx(out=x_codes[0][:].bitcast(FP8X4), scales=x_scales[0][:], in_=picked0)
        gather_shared_pair(1)
        gather_plane(1, 2)
        gather_plane(1, 3)
        picked1 = picked[1][:].rearrange("p s j -> p (s j)")
        w_bf = {(i, g): round_w(i, g) for i in (SCORE_W, VALUE_W) for g in range(PASSES)}
        x_codes[1] = keep.tile([P, S], U32, name="x_codes1", align_bytes=64, tag="zero0")
        x_scales[1] = keep.tile([P, S], U8, name="x_scales1", align_bytes=64)
        w_mx = {}

        def quantize_x1(q):
            cols = slice(q * SP, (q + 1) * SP)
            nc.vector.quantize_mx(
                out=x_codes[1][:, cols].bitcast(FP8X4),
                scales=x_scales[1][:, cols],
                in_=picked1[:, q * SP * PACK : (q + 1) * SP * PACK],
            )

        def quantize_w(i, g):
            codes = keep.tile([P, N], U32, name="w_codes%d_%d" % (i, g), align_bytes=64)
            scales = keep.tile([P, N], U8, name="w_scales%d_%d" % (i, g), align_bytes=64)
            nc.vector.quantize_mx(out=codes[:].bitcast(FP8X4), scales=scales[:], in_=w_bf[i, g])
            w_mx[i, g] = (codes, scales)

        score = [psum.tile([P, SP], F32, name="score%d" % q) for q in range(PARTS)]
        value = [psum.tile([P, SH], F32, name="value%d" % h) for h in range(HALVES)]

        def product(bank, i, g, first_col, opens):
            cols = slice(first_col, first_col + bank.shape[1])
            nc.tensor.matmul_mx(
                out=bank[:],
                lhsT=w_mx[i, g][0][:].bitcast(FP8X4),
                lhsT_scale=w_mx[i, g][1][:],
                rhs=x_codes[g][:, cols].bitcast(FP8X4),
                rhs_scale=x_scales[g][:, cols],
                start=opens,
                stop=not opens,
            )

        quantize_w(SCORE_W, 0)
        for q in range(PH):
            product(score[q], SCORE_W, 0, q * SP, True)
        quantize_w(SCORE_W, 1)
        for q in range(PARTS):
            quantize_x1(q)
            if q < PH:
                product(score[q], SCORE_W, 1, q * SP, False)
            else:
                product(score[q], SCORE_W, 1, q * SP, True)
                product(score[q], SCORE_W, 0, q * SP, False)

        e = [keep.tile([P, PH, VP, D], F32, name="e%d" % h) for h in range(HALVES)]
        top = {}

        shifted = {}

        def largest(q):
            nc.vector.tensor_reduce(
                out=top[q], in_=score[q][:].rearrange("p (d u) -> p u d", d=D), axis=AX.X, op=ALU.max
            )

        def exponential(q):
            nc.vector.tensor_tensor(
                out=shifted[q],
                in0=score[q][:].rearrange("p (d u) -> p u d", d=D),
                in1=top[q].unsqueeze(2).to_broadcast([P, VP, D]),
                op=ALU.subtract,
            )
            nc.scalar.activation(out=e[q // PH][:, q % PH], in_=shifted[q], func=ACT.Exp)

        quantize_w(VALUE_W, 0)
        product(value[0], VALUE_W, 0, 0, True)
        tops0 = keep.tile([P, PH, VP], F32, name="tops0", align_bytes=64)
        top[0], top[1] = tops0[:, 0], tops0[:, 1]
        largest(0)
        largest(1)
        quantize_w(VALUE_W, 1)
        held = keep.tile([P, PH, D + 1, VP], F32, name="held", align_bytes=64, tag="zero1")
        shifted1 = keep.tile([P, PH, VP, D], F32, name="shifted1", align_bytes=64)
        for q in range(PH):
            shifted[q] = held[:, q, :D].rearrange("p a b -> p (a b)").rearrange("p (u d) -> p u d", d=D)
            shifted[PH + q], top[PH + q] = shifted1[:, q], held[:, q, D]
        exponential(0)
        exponential(1)
        product(value[0], VALUE_W, 1, 0, False)
        product(value[1], VALUE_W, 1, SH, True)
        product(value[1], VALUE_W, 0, SH, False)
        largest(2)
        largest(3)
        exponential(2)
        exponential(3)

        den_other = keep.tile([P, HALVES, VH], F32, name="den_other")
        num = keep.tile([P, HALVES, VH], F32, name="num")
        weighted = [keep.tile([P, PH, VP, D], F32, name="weighted%d" % h) for h in range(HALVES)]

        nc.vector.tensor_reduce(
            out=den_other[:, 1], in_=e[0][:].rearrange("p q u d -> p (q u) d"), axis=AX.X, op=ALU.add
        )
        nc.vector.tensor_tensor(
            out=weighted[0][:],
            in0=value[0][:].rearrange("p (q d u) -> p q u d", q=PH, d=D),
            in1=e[0][:],
            op=ALU.mult,
        )
        by_place = weighted[0][:].rearrange("p q u d -> p (q u) d")
        pair_sums = keep.tile([P, VH, 2], F32, name="pair_sums")
        nc.gpsimd.tensor_tensor(out=pair_sums[:], in0=by_place[:, :, 0:2], in1=by_place[:, :, 2:4], op=ALU.add)
        nc.gpsimd.tensor_tensor(out=num[:, 0], in0=pair_sums[:, :, 0], in1=pair_sums[:, :, 1], op=ALU.add)

        for q in range(PH):
            nc.vector.tensor_reduce(
                out=den_other[:, 0, q * VP : (q + 1) * VP], in_=e[1][:, q], axis=AX.X, op=ALU.add
            )
        for q in range(PH):
            nc.vector.tensor_tensor(
                out=weighted[1][:, q],
                in0=value[1][:, q * SP : (q + 1) * SP].rearrange("p (d u) -> p u d", d=D),
                in1=e[1][:, q],
                op=ALU.mult,
            )
        den_both = keep.tile([P, VH], F32, name="den_both")
        nc.vector.tensor_reduce(
            out=den_both[:], in_=den_other[:].rearrange("p h v -> p v h"), axis=AX.X, op=ALU.mult
        )
        for q in range(PH):
            nc.vector.tensor_reduce(
                out=num[:, 1, q * VP : (q + 1) * VP], in_=weighted[1][:, q], axis=AX.X, op=ALU.add
            )
        rec = keep.tile([P, VH], F32, name="rec")
        nc.vector.reciprocal(out=rec[:], in_=den_both[:])

        cross = keep.tile([P, HALVES, VH], F32, name="cross")
        res = keep.tile([P, HALVES, VH], F32, name="res", tag="pair_sums")
        for h in reversed(range(HALVES)):
            nc.vector.tensor_tensor(out=cross[:, h], in0=num[:, h], in1=den_other[:, h], op=ALU.mult)
        for h in reversed(range(HALVES)):
            nc.vector.tensor_tensor(out=res[:, h], in0=cross[:, h], in1=rec[:], op=ALU.mult)
        nc.sync.dma_start(out=out, in_=res[:].rearrange("p h v -> p (h v)"))
